import numpy as np
import ml_dtypes


def mxq(x, axis, fmt="e4m3"):
    dtype, down = {"e4m3": (ml_dtypes.float8_e4m3fn, 7), "e5m2": (ml_dtypes.float8_e5m2, 14)}[fmt]
    v = np.moveaxis(np.asarray(x, np.float32).astype(ml_dtypes.bfloat16).astype(np.float64), axis, -1)
    blocks = v.reshape(v.shape[:-1] + (-1, 32))
    amax = np.abs(blocks).max(-1, keepdims=True)
    byte = np.maximum(np.where(amax > 0, np.frexp(amax)[1] - 1 + 127, 0) - down, 1)
    scale = np.exp2(byte - 127.0)
    codes = (blocks / scale).astype(np.float32).astype(dtype).astype(np.float64)
    return np.moveaxis((codes * scale).reshape(v.shape), -1, axis)


WIDE = False


def mx_kscale(k):
    if not WIDE:
        return np.ones(k)
    levels = np.array([10, -10, 5, -5, 0])
    if k % 512:
        return np.exp2(np.random.permutation(np.resize(levels, k // 32))).repeat(32)
    a = np.empty((k // 512, 16))
    for p in range(k // 512):
        a[p, :8] = np.random.permutation(np.resize(levels, 8))
        for g in range(8):
            far = levels[np.abs(levels - a[p, g]) >= 10]
            a[p, g + 8] = far[np.random.randint(len(far))]
    return np.exp2(a.ravel()).repeat(32)


def f64(x):
    return np.asarray(x).astype(np.float64)


def striped(idx):
    return np.tile(np.asarray(idx).reshape(-1, 16).T, (8, 1)).astype(np.uint16)


def unstriped(offs):
    return offs[:16].T.reshape(-1).astype(np.int64)


E2M1 = np.array([0.0, 0.5, 1.0, 1.5, 2.0, 3.0, 4.0, 6.0, -0.0, -0.5, -1.0, -1.5, -2.0, -3.0, -4.0, -6.0])


def pack_weight(w, fmt):
    k, n = w.shape
    w = f64(np.asarray(w, np.float32).astype(ml_dtypes.bfloat16)).reshape(k // 32, 32, n)
    amax = np.abs(w).max(1)
    if fmt == "e4m3":
        byte = np.frexp(amax)[1] - 1 + 127 - 7
    else:
        mant, ex = np.frexp(amax / 6.0)
        byte = np.where(mant > 0.5, ex, ex - 1) + 127
    byte = np.clip(np.where(amax > 0, byte, 1), 1, 254)
    scaled = (w * np.exp2(127.0 - byte)[:, None, :]).reshape(k, n).astype(np.float32)
    by_word = np.ascontiguousarray(scaled.reshape(k // 512, 128, 4, n).transpose(0, 1, 3, 2))
    if fmt == "e4m3":
        words = by_word.astype(ml_dtypes.float8_e4m3fn).view(np.uint8)
    else:
        c = by_word.astype(ml_dtypes.float4_e2m1fn).view(np.uint8) & 0xF
        words = (c[..., 0::2] | (c[..., 1::2] << 4)).reshape(k // 512, 128, 2 * n)
    return np.ascontiguousarray(words), np.ascontiguousarray(byte.astype(np.uint8).reshape(k // 512, 16, n))


def unpack_weight(words, scales, fmt):
    g, _, n = scales.shape
    words = np.ascontiguousarray(words).reshape(g, 128, n, -1)
    if fmt == "e4m3":
        vals = words.view(ml_dtypes.float8_e4m3fn).astype(np.float64)
    else:
        nib = np.empty((g, 128, n, 4), np.uint8)
        nib[..., 0::2] = words & 0xF
        nib[..., 1::2] = words >> 4
        vals = E2M1[nib]
    vals = vals * np.repeat(np.exp2(scales.astype(np.float64) - 127.0), 8, axis=1)[..., None]
    return vals.transpose(0, 1, 3, 2).reshape(g * 512, n)


def bf(x):
    return np.asarray(x, np.float32).astype(ml_dtypes.bfloat16)


def planes(Y):
    r, m = Y.shape
    b = f64(bf(Y)).reshape(r // 32, 32, m)
    amax = np.abs(b).max(1)
    byte = np.clip(np.where(amax > 0, np.frexp(amax)[1] - 1 + 127 - 7, 1), 1, 254)
    codes = (b * np.exp2(127.0 - byte)[:, None, :]).reshape(r, m).astype(np.float32).astype(ml_dtypes.float8_e4m3fn).view(np.uint8)
    words = codes.reshape(r // 512, 128, 4, m).transpose(0, 1, 3, 2)
    return np.ascontiguousarray(words), np.ascontiguousarray(byte.astype(np.uint8).reshape(r // 512, 16, m))


D, T, I, Q, E, Z, X = 512, 2048, 512, 256, 512, 1024, 1024


def setup_inputs():
    n = np.random.standard_normal
    idx = np.random.permutation(T)[:I]
    idx2 = np.random.permutation(Z)[:I]
    idx3 = np.random.permutation(Z)[:I]
    idx4 = np.random.permutation(X)[:I]
    fd = mx_kscale(D)
    fi = mx_kscale(I)
    keysp = pack_weight(n((D, T)) / fd[:, None], "e2m1")
    return {
        "query": (n((D, Q)) * 1.0 / np.sqrt(D) * fd[:, None]).astype(np.float32),
        "keys_words": keysp[0],
        "keys_scales": keysp[1],
        "os": (np.random.uniform(0.02, 0.08, (1, I)) * fi).astype(np.float32),
        "vals": (n((E, T))).astype(np.float32),
        "vals2": (n((E, X))).astype(np.float32),
        "vsc": (np.random.uniform(0.5, 2.0, (1, I)) / fi).astype(np.float32),
        "offs": striped(idx),
        "offs2": striped(idx2),
        "offs3": striped(idx3),
        "offs4": striped(idx4),
    }


def reference(query, keys_words, keys_scales, os, vals, vals2, vsc, offs, offs2, offs3, offs4):
    idx = unstriped(offs)
    idx2 = unstriped(offs2)
    idx3 = unstriped(offs3)
    idx4 = unstriped(offs4)
    keysu = unpack_weight(keys_words, keys_scales, "e2m1")
    queryq = mxq(f64(query), 0, "e4m3")
    keysidxg = keysu[:, idx]
    a = queryq.T @ keysidxg
    f0 = np.zeros((Q, Z))
    f0[:, idx2] = a
    w = a + f0[:, idx3]
    wo1 = w * f64(os)
    wt1 = wo1.T
    vz = np.abs(f64(vals)[:, idx] - f64(vals2)[:, idx4]) * f64(vsc)
    vt1 = vz.T
    vt1q = mxq(vt1, 0, "e4m3")
    wt1q = mxq(wt1, 0, "e4m3")
    o = vt1q.T @ wt1q
    words, scales = planes(o)
    return o, words, scales

@@ -1,0 +1,210 @@
+from contextlib import ExitStack
+
+import concourse.mybir as mybir
+from concourse.masks import make_identity
+
+D, T, I, Q, E, Z, X = 512, 2048, 512, 256, 512, 1024, 1024
+FLOPS = 2 * D * Q * I + 2 * I * E * Q
+
+F32 = mybir.dt.float32
+BF16 = mybir.dt.bfloat16
+I32 = mybir.dt.int32
+U32 = mybir.dt.uint32
+U16 = mybir.dt.uint16
+U8 = mybir.dt.uint8
+FP8X4 = mybir.dt.float8_e4m3fn_x4
+FP4X4 = mybir.dt.float4_e2m1fn_x4
+MULT = mybir.AluOpType.mult
+COPY = mybir.ActivationFunctionType.Copy
+ABS = mybir.ActivationFunctionType.Abs
+
+P = 128
+PACK = 4
+HALVES = Q // P
+
+
+def tile_attend_passedthrough_apartvalues_lean_pl_kernel(
+    tc, query, keys_words, keys_scales, wfac, vals, vals2, vsc, offs, offs2, offs3, offs4, out_0, out_1, out_2
+):
+    nc = tc.nc
+    with ExitStack() as ctx:
+        sb = ctx.enter_context(tc.tile_pool(name="sb", bufs=1))
+        ps = ctx.enter_context(tc.psum_pool(name="ps", bufs=1))
+
+        def tile(shape, dtype, name, over=None):
+            return sb.tile(shape, dtype, name=name, tag=over or name, align_bytes=64)
+
+        def load_list(src, name):
+            lst = tile([P, I // 16], U16, name)
+            nc.sync.dma_start(lst[:], src)
+            return lst
+
+        def turn(bank, src_of, first, last):
+            for t in range(PACK):
+                nc.tensor.matmul(
+                    bank[:, t, :], lhsT=src_of(t), rhs=ident[:], is_transpose=True,
+                    start=(first and t == 0), stop=(last and t == PACK - 1),
+                )
+
+        ks_pool = tile([P, T], U8, "ks_pool")
+        nc.vector.memset(ks_pool[:].bitcast(U32), 0)
+        by_tok = load_list(offs, "by_tok")
+        kw_pool = tile([P, T], U16, "kw_pool")
+        nc.sync.dma_start(kw_pool[:].bitcast(I32), keys_words[0].bitcast(I32))
+        for quad in range(4):
+            nc.sync.dma_start(
+                ks_pool[32 * quad : 32 * quad + 4, :].bitcast(I32),
+                keys_scales[0, 4 * quad : 4 * quad + 4, :].bitcast(I32),
+            )
+        q_raw = tile([P, PACK, Q], F32, "q_raw")
+        nc.sync.dma_start(q_raw[:], query.rearrange("(p t) q -> p t q", t=PACK))
+
+        vals_rows = vals.rearrange("(m j) c -> j m c", j=PACK)
+        vals2_rows = vals2.rearrange("(m j) c -> j m c", j=PACK)
+        v1_pool = [tile([P, T], F32, f"v1_pool{j}") for j in range(PACK)]
+        v2_pool = [tile([P, X], F32, f"v2_pool{j}") for j in range(PACK)]
+        by_col = load_list(offs4, "by_col")
+        nc.sync.dma_start(v2_pool[0][:], vals2_rows[0])
+        put_at = load_list(offs2, "put_at")
+        nc.sync.dma_start(v1_pool[0][:], vals_rows[0])
+        look_at = load_list(offs3, "look_at")
+        nc.sync.dma_start(v2_pool[1][:], vals2_rows[1])
+        w_fac = tile([P, PACK], F32, "w_fac")
+        v_fac = tile([P, PACK], F32, "v_fac")
+        nc.sync.dma_start(w_fac[:], wfac.rearrange("o (p t) -> (o p) t", t=PACK))
+        nc.sync.dma_start(v_fac[:], vsc.rearrange("o (p t) -> (o p) t", t=PACK))
+        nc.sync.dma_start(v1_pool[1][:], vals_rows[1])
+        for j in range(2, PACK):
+            nc.sync.dma_start(v2_pool[j][:], vals2_rows[j])
+            nc.sync.dma_start(v1_pool[j][:], vals_rows[j])
+
+        places = [tile([P, Z], F32, f"places{h}") for h in range(HALVES)]
+        nc.vector.memset(places[0][:], 0.0)
+        nc.gpsimd.memset(places[1][:], 0.0)
+        ident = tile([P, P], F32, "ident")
+        make_identity(nc, ident[:])
+
+        kw = tile([P, I], U16, "kw")
+        ks = tile([P, I], U8, "ks")
+        q_bf = tile([P, Q, PACK], BF16, "q_bf")
+        q_codes = tile([P, Q], U32, "q_codes")
+        q_scales = tile([P, Q], U8, "q_scales")
+        nc.vector.tensor_copy(kw[:], kw_pool[:].indirect(by_tok[:]))
+        nc.vector.tensor_copy(ks[:], ks_pool[:].indirect(by_tok[:]))
+        score_bank = [ps.tile([P, I], F32, name=f"score_bank{h}", tag=f"v_bank{h}") for h in range(HALVES)]
+        score = [tile([P, I], F32, f"score{h}") for h in range(HALVES)]
+        for h in range(HALVES):
+            cols = slice(h * P, (h + 1) * P)
+            nc.scalar.copy(q_bf[:, cols, :], q_raw[:, :, cols].rearrange("p t q -> p q t"))
+            nc.vector.quantize_mx(
+                out=q_codes[:, cols].bitcast(FP8X4), scales=q_scales[:, cols],
+                in_=q_bf[:, cols, :].rearrange("p q t -> p (q t)"),
+            )
+            nc.tensor.matmul_mx(
+                out=score_bank[h][:], lhsT=q_codes[:, cols].bitcast(FP8X4), lhsT_scale=q_scales[:, cols],
+                rhs=kw[:].bitcast(FP4X4), rhs_scale=ks[:], start=True, stop=True,
+            )
+        nc.vector.tensor_copy(score[0][:], score_bank[0][:])
+        nc.scalar.copy(score[1][:], score_bank[1][:])
+
+        nc.vector.tensor_copy(places[0][:].indirect(put_at[:]), score[0][:])
+        for s in range(2):
+            nc.scalar.activation(
+                places[1][:].indirect(put_at[:, 16 * s : 16 * (s + 1)]), score[1][:, 256 * s : 256 * (s + 1)], COPY
+            )
+        w_bank = [ps.tile([P, PACK, P], F32, name=f"w_bank{h}") for h in range(HALVES)]
+        for h in range(HALVES):
+            turn(w_bank[h], lambda t: score[h][:, t:I:PACK], True, False)
+
+        v_bank = [ps.tile([P, PACK, P], F32, name=f"v_bank{j}", tag=f"v_bank{j}") for j in range(PACK)]
+        v_codes = tile([P, E], U32, "v_codes")
+        v_scales = tile([P, E], U8, "v_scales")
+
+        def gather_values(j):
+            neg2 = tile([P, I], F32, f"neg2_{j}")
+            nc.scalar.activation(neg2[:], v2_pool[j][:].indirect(by_col[:]), COPY, scale=-1.0)
+            turn(v_bank[j], lambda t: neg2[:, t:I:PACK], True, False)
+            pos1 = tile([P, PACK, P], F32, f"pos1_{j}")
+            nc.vector.tensor_copy(pos1[:].rearrange("p t s -> p s t"), v1_pool[j][:].indirect(by_tok[:]))
+            turn(v_bank[j], lambda t: pos1[:, t, :], False, True)
+
+        def quantise_values(j0, j1):
+            n = (j1 - j0) * P
+            last = j1 == PACK
+            apart = tile([P, n, PACK], F32, f"apart{j0}", None if last else f"v2_pool{j1}")
+            for j in range(j0, j1):
+                nc.scalar.activation(
+                    apart[:, (j - j0) * P : (j - j0 + 1) * P, :], v_bank[j][:].rearrange("p t m -> p m t"), ABS
+                )
+            v_bf = tile([P, n, PACK], BF16, f"v_bf{j0}", None if last else f"v1_pool{j1}")
+            nc.vector.tensor_tensor(v_bf[:], apart[:], v_fac[:].unsqueeze(1).to_broadcast([P, n, PACK]), MULT)
+            nc.vector.quantize_mx(
+                out=v_codes[:, j0 * P : j1 * P].bitcast(FP8X4), scales=v_scales[:, j0 * P : j1 * P],
+                in_=v_bf[:].rearrange("p m t -> p (m t)"),
+            )
+
+        found0 = tile([P, PACK, P], F32, "found0")
+        nc.vector.tensor_copy(found0[:].rearrange("p t s -> p s t"), places[0][:].indirect(look_at[:]))
+        turn(w_bank[0], lambda t: found0[:, t, :], False, True)
+        found1 = tile([P, I], F32, "found1")
+        nc.scalar.activation(found1[:], places[1][:].indirect(look_at[:]), COPY)
+        turn(w_bank[1], lambda t: found1[:, t:I:PACK], False, True)
+
+        gather_values(0)
+        gather_values(1)
+
+        w_bf = tile([P, Q, PACK], BF16, "w_bf", "v1_pool1")
+        w_codes = tile([P, Q], U32, "w_codes")
+        w_scales = tile([P, Q], U8, "w_scales")
+        for h in range(HALVES):
+            nc.vector.tensor_tensor(
+                w_bf[:, h * P : (h + 1) * P, :], w_bank[h][:].rearrange("p t q -> p q t"),
+                w_fac[:].unsqueeze(1).to_broadcast([P, P, PACK]), MULT,
+            )
+        nc.vector.quantize_mx(
+            out=w_codes[:].bitcast(FP8X4), scales=w_scales[:], in_=w_bf[:].rearrange("p q t -> p (q t)")
+        )
+
+        out_bank = [ps.tile([P, PACK, P], F32, name=f"out_bank{h}", tag=f"v_bank{2 - h}") for h in range(HALVES)]
+
+        def product(j):
+            for h in range(HALVES):
+                cols = slice(h * P, (h + 1) * P)
+                nc.tensor.matmul_mx(
+                    out=out_bank[h][:, j, :], lhsT=v_codes[:, j * P : (j + 1) * P].bitcast(FP8X4),
+                    lhsT_scale=v_scales[:, j * P : (j + 1) * P],
+                    rhs=w_codes[:, cols].bitcast(FP8X4), rhs_scale=w_scales[:, cols], start=True, stop=True,
+                )
+
+        out_rows = out_0.rearrange("(m j) q -> m j q", j=PACK)
+        early = tile([P, PACK - 1, Q], F32, "early")
+        late = tile([P, Q], F32, "late")
+        gather_values(2)
+        quantise_values(0, 2)
+        gather_values(3)
+        quantise_values(2, 3)
+        for j in range(PACK - 1):
+            product(j)
+        quantise_values(3, 4)
+        for h in range(HALVES):
+            nc.scalar.copy(early[:, :, h * P : (h + 1) * P], out_bank[h][:, : PACK - 1, :])
+        nc.sync.dma_start(out_rows[:, : PACK - 1, :], early[:])
+        product(PACK - 1)
+
+        o_bf = tile([P, Q, PACK], BF16, "o_bf")
+        o_codes = tile([P, Q], U32, "o_codes")
+        o_scales = tile([P, Q], U8, "o_scales")
+        nc.vector.tensor_copy(o_bf[:, :P, :], out_bank[0][:].rearrange("p j q -> p q j"))
+        nc.scalar.copy(o_bf[:, P:, :], out_bank[1][:].rearrange("p j q -> p q j"))
+        nc.vector.quantize_mx(
+            out=o_codes[:].bitcast(FP8X4), scales=o_scales[:], in_=o_bf[:].rearrange("p q j -> p (q j)")
+        )
+        for h in (1, 0):
+            nc.scalar.copy(late[:, h * P : (h + 1) * P], out_bank[h][:, PACK - 1, :])
+        nc.sync.dma_start(out_1[0].rearrange("p c r -> p (c r)").bitcast(I32), o_codes[:].bitcast(I32))
+        nc.scalar.dma_start(out_rows[:, PACK - 1, :], late[:])
+        for quad in range(4):
+            nc.sync.dma_start(
+                out_2[0, 4 * quad : 4 * quad + 4, :].bitcast(I32),
+                o_scales[32 * quad : 32 * quad + 4, :].bitcast(I32),
+            )

@@ -15,6 +15,7 @@ U8 = mybir.dt.uint8
 FP8X4 = mybir.dt.float8_e4m3fn_x4
 FP4X4 = mybir.dt.float4_e2m1fn_x4
 MULT = mybir.AluOpType.mult
+SUBTRACT = mybir.AluOpType.subtract
 COPY = mybir.ActivationFunctionType.Copy
 ABS = mybir.ActivationFunctionType.Abs
 
@@ -91,7 +92,7 @@ def tile_attend_passedthrough_apartvalues_lean_pl_kernel(
         q_scales = tile([P, Q], U8, "q_scales")
         nc.vector.tensor_copy(kw[:], kw_pool[:].indirect(by_tok[:]))
         nc.vector.tensor_copy(ks[:], ks_pool[:].indirect(by_tok[:]))
-        score_bank = [ps.tile([P, I], F32, name=f"score_bank{h}", tag=f"v_bank{h}") for h in range(HALVES)]
+        score_bank = [ps.tile([P, I], F32, name=f"score_bank{h}", tag=f"mx_bank{h}") for h in range(HALVES)]
         score = [tile([P, I], F32, f"score{h}") for h in range(HALVES)]
         for h in range(HALVES):
             cols = slice(h * P, (h + 1) * P)
@@ -120,24 +121,29 @@ def tile_attend_passedthrough_apartvalues_lean_pl_kernel(
         v_codes = tile([P, E], U32, "v_codes")
         v_scales = tile([P, E], U8, "v_scales")
 
-        def gather_values(j):
-            neg2 = tile([P, I], F32, f"neg2_{j}")
-            nc.scalar.activation(neg2[:], v2_pool[j][:].indirect(by_col[:]), COPY, scale=-1.0)
-            turn(v_bank[j], lambda t: neg2[:, t:I:PACK], True, False)
-            pos1 = tile([P, PACK, P], F32, f"pos1_{j}")
-            nc.vector.tensor_copy(pos1[:].rearrange("p t s -> p s t"), v1_pool[j][:].indirect(by_tok[:]))
-            turn(v_bank[j], lambda t: pos1[:, t, :], False, True)
+        diff = []
 
-        def quantise_values(j0, j1):
-            n = (j1 - j0) * P
-            last = j1 == PACK
-            apart = tile([P, n, PACK], F32, f"apart{j0}", None if last else f"v2_pool{j1}")
+        def gather_values(j):
+            second = tile([P, I], F32, f"second{j}")
+            nc.scalar.activation(second[:], v2_pool[j][:].indirect(by_col[:]), COPY)
+            diff.append(tile([P, I], F32, f"diff{j}", "places0" if j == 0 else None))
+            nc.vector.tensor_tensor(diff[j][:], v1_pool[j][:].indirect(by_tok[:]), second[:], SUBTRACT)
+
+        def turn_values(j0, j1, over):
+            apart = tile([P, j1 - j0, PACK, P], F32, f"apart{j0}", over)
             for j in range(j0, j1):
                 nc.scalar.activation(
-                    apart[:, (j - j0) * P : (j - j0 + 1) * P, :], v_bank[j][:].rearrange("p t m -> p m t"), ABS
+                    apart[:, j - j0].rearrange("p t s -> p s t"), diff[j][:].rearrange("p (s t) -> p s t", t=PACK), ABS
                 )
-            v_bf = tile([P, n, PACK], BF16, f"v_bf{j0}", None if last else f"v1_pool{j1}")
-            nc.vector.tensor_tensor(v_bf[:], apart[:], v_fac[:].unsqueeze(1).to_broadcast([P, n, PACK]), MULT)
+                turn(v_bank[j], lambda t: apart[:, j - j0, t, :], True, True)
+
+        def quantise_values(j0, j1):
+            v_bf = tile([P, (j1 - j0) * P, PACK], BF16, f"v_bf{j0}", "v1_pool3")
+            for j in range(j0, j1):
+                nc.vector.tensor_tensor(
+                    v_bf[:, (j - j0) * P : (j - j0 + 1) * P, :], v_bank[j][:].rearrange("p t m -> p m t"),
+                    v_fac[:].unsqueeze(1).to_broadcast([P, P, PACK]), MULT,
+                )
             nc.vector.quantize_mx(
                 out=v_codes[:, j0 * P : j1 * P].bitcast(FP8X4), scales=v_scales[:, j0 * P : j1 * P],
                 in_=v_bf[:].rearrange("p m t -> p (m t)"),
@@ -153,7 +159,7 @@ def tile_attend_passedthrough_apartvalues_lean_pl_kernel(
         gather_values(0)
         gather_values(1)
 
-        w_bf = tile([P, Q, PACK], BF16, "w_bf", "v1_pool1")
+        w_bf = tile([P, Q, PACK], BF16, "w_bf")
         w_codes = tile([P, Q], U32, "w_codes")
         w_scales = tile([P, Q], U8, "w_scales")
         for h in range(HALVES):
@@ -165,11 +171,11 @@ def tile_attend_passedthrough_apartvalues_lean_pl_kernel(
             out=w_codes[:].bitcast(FP8X4), scales=w_scales[:], in_=w_bf[:].rearrange("p q t -> p (q t)")
         )
 
-        out_bank = [ps.tile([P, PACK, P], F32, name=f"out_bank{h}", tag=f"v_bank{2 - h}") for h in range(HALVES)]
+        out_bank = [ps.tile([P, PACK, P], F32, name=f"out_bank{h}", tag=f"mx_bank{h}") for h in range(HALVES)]
 
-        def product(j):
-            for h in range(HALVES):
-                cols = slice(h * P, (h + 1) * P)
+        def product(j0, j1, h):
+            cols = slice(h * P, (h + 1) * P)
+            for j in range(j0, j1):
                 nc.tensor.matmul_mx(
                     out=out_bank[h][:, j, :], lhsT=v_codes[:, j * P : (j + 1) * P].bitcast(FP8X4),
                     lhsT_scale=v_scales[:, j * P : (j + 1) * P],
@@ -177,34 +183,37 @@ def tile_attend_passedthrough_apartvalues_lean_pl_kernel(
                 )
 
         out_rows = out_0.rearrange("(m j) q -> m j q", j=PACK)
-        early = tile([P, PACK - 1, Q], F32, "early")
-        late = tile([P, Q], F32, "late")
+        early = tile([P, 2, Q], F32, "early")
+        late = tile([P, 2, Q], F32, "late")
         gather_values(2)
-        quantise_values(0, 2)
+        turn_values(0, 1, "v2_pool2")
         gather_values(3)
-        quantise_values(2, 3)
-        for j in range(PACK - 1):
-            product(j)
-        quantise_values(3, 4)
+        turn_values(1, 3, "v2_pool3")
+        turn_values(3, 4, None)
+        quantise_values(0, 2)
+        quantise_values(2, 4)
         for h in range(HALVES):
-            nc.scalar.copy(early[:, :, h * P : (h + 1) * P], out_bank[h][:, : PACK - 1, :])
-        nc.sync.dma_start(out_rows[:, : PACK - 1, :], early[:])
-        product(PACK - 1)
+            product(0, 2, h)
+            nc.scalar.copy(early[:, :, h * P : (h + 1) * P], out_bank[h][:, :2, :])
+        nc.sync.dma_start(out_rows[:, :2, :], early[:])
+        for h in range(HALVES):
+            product(2, 4, h)
 
         o_bf = tile([P, Q, PACK], BF16, "o_bf")
         o_codes = tile([P, Q], U32, "o_codes")
         o_scales = tile([P, Q], U8, "o_scales")
         nc.vector.tensor_copy(o_bf[:, :P, :], out_bank[0][:].rearrange("p j q -> p q j"))
         nc.scalar.copy(o_bf[:, P:, :], out_bank[1][:].rearrange("p j q -> p q j"))
+        nc.vector.tensor_copy(late[:, :, :P], out_bank[0][:, 2:, :])
+        nc.scalar.copy(late[:, :, P:], out_bank[1][:, 2:, :])
         nc.vector.quantize_mx(
             out=o_codes[:].bitcast(FP8X4), scales=o_scales[:], in_=o_bf[:].rearrange("p q j -> p (q j)")
         )
-        for h in (1, 0):
-            nc.scalar.copy(late[:, h * P : (h + 1) * P], out_bank[h][:, PACK - 1, :])
-        nc.sync.dma_start(out_1[0].rearrange("p c r -> p (c r)").bitcast(I32), o_codes[:].bitcast(I32))
-        nc.scalar.dma_start(out_rows[:, PACK - 1, :], late[:])
+        nc.sync.dma_start(out_rows[:, 2:, :], late[:])
+        nc.scalar.dma_start(out_1[0].rearrange("p c r -> p (c r)").bitcast(I32), o_codes[:].bitcast(I32))
         for quad in range(4):
-            nc.sync.dma_start(
+            queue = nc.sync if quad < 3 else nc.scalar
+            queue.dma_start(
                 out_2[0, 4 * quad : 4 * quad + 4, :].bitcast(I32),
                 o_scales[32 * quad : 32 * quad + 4, :].bitcast(I32),
             )

@@ -15,7 +15,6 @@ U8 = mybir.dt.uint8
 FP8X4 = mybir.dt.float8_e4m3fn_x4
 FP4X4 = mybir.dt.float4_e2m1fn_x4
 MULT = mybir.AluOpType.mult
-SUBTRACT = mybir.AluOpType.subtract
 COPY = mybir.ActivationFunctionType.Copy
 ABS = mybir.ActivationFunctionType.Abs
 
@@ -30,6 +29,7 @@ def tile_attend_passedthrough_apartvalues_lean_pl_kernel(
     nc = tc.nc
     with ExitStack() as ctx:
         sb = ctx.enter_context(tc.tile_pool(name="sb", bufs=1))
+        last = ctx.enter_context(tc.tile_pool(name="last", bufs=1))
         ps = ctx.enter_context(tc.psum_pool(name="ps", bufs=1))
 
         def tile(shape, dtype, name, over=None):
@@ -62,21 +62,23 @@ def tile_attend_passedthrough_apartvalues_lean_pl_kernel(
 
         vals_rows = vals.rearrange("(m j) c -> j m c", j=PACK)
         vals2_rows = vals2.rearrange("(m j) c -> j m c", j=PACK)
-        v1_pool = [tile([P, T], F32, f"v1_pool{j}") for j in range(PACK)]
+        v1_pool = [tile([P, T], F32, f"v1_pool{j}") for j in range(PACK - 1)]
+        v1_pool.append(last.tile([P, T], F32, name="v1_pool3", offset=0, align_bytes=64))
         v2_pool = [tile([P, X], F32, f"v2_pool{j}") for j in range(PACK)]
         by_col = load_list(offs4, "by_col")
         nc.sync.dma_start(v2_pool[0][:], vals2_rows[0])
+        nc.sync.dma_start(v2_pool[1][:], vals2_rows[1])
         put_at = load_list(offs2, "put_at")
         nc.sync.dma_start(v1_pool[0][:], vals_rows[0])
         look_at = load_list(offs3, "look_at")
-        nc.sync.dma_start(v2_pool[1][:], vals2_rows[1])
-        w_fac = tile([P, PACK], F32, "w_fac")
-        v_fac = tile([P, PACK], F32, "v_fac")
-        nc.sync.dma_start(w_fac[:], wfac.rearrange("o (p t) -> (o p) t", t=PACK))
-        nc.sync.dma_start(v_fac[:], vsc.rearrange("o (p t) -> (o p) t", t=PACK))
         nc.sync.dma_start(v1_pool[1][:], vals_rows[1])
-        for j in range(2, PACK):
+        w_fac = tile([P, PACK], F32, "w_fac")
+        nc.sync.dma_start(w_fac[:], wfac.rearrange("o (p t) -> (o p) t", t=PACK))
+        for j in (2, 3):
             nc.sync.dma_start(v2_pool[j][:], vals2_rows[j])
+        v_fac = tile([P, PACK], F32, "v_fac")
+        nc.sync.dma_start(v_fac[:], vsc.rearrange("o (p t) -> (o p) t", t=PACK))
+        for j in (2, 3):
             nc.sync.dma_start(v1_pool[j][:], vals_rows[j])
 
         places = [tile([P, Z], F32, f"places{h}") for h in range(HALVES)]
@@ -92,7 +94,7 @@ def tile_attend_passedthrough_apartvalues_lean_pl_kernel(
         q_scales = tile([P, Q], U8, "q_scales")
         nc.vector.tensor_copy(kw[:], kw_pool[:].indirect(by_tok[:]))
         nc.vector.tensor_copy(ks[:], ks_pool[:].indirect(by_tok[:]))
-        score_bank = [ps.tile([P, I], F32, name=f"score_bank{h}", tag=f"mx_bank{h}") for h in range(HALVES)]
+        score_bank = [ps.tile([P, I], F32, name=f"score_bank{h}", tag=f"v_bank{h}") for h in range(HALVES)]
         score = [tile([P, I], F32, f"score{h}") for h in range(HALVES)]
         for h in range(HALVES):
             cols = slice(h * P, (h + 1) * P)
@@ -106,47 +108,40 @@ def tile_attend_passedthrough_apartvalues_lean_pl_kernel(
                 rhs=kw[:].bitcast(FP4X4), rhs_scale=ks[:], start=True, stop=True,
             )
         nc.vector.tensor_copy(score[0][:], score_bank[0][:])
-        nc.scalar.copy(score[1][:], score_bank[1][:])
+        nc.vector.tensor_copy(score[1][:], score_bank[1][:])
 
         nc.vector.tensor_copy(places[0][:].indirect(put_at[:]), score[0][:])
         for s in range(2):
             nc.scalar.activation(
                 places[1][:].indirect(put_at[:, 16 * s : 16 * (s + 1)]), score[1][:, 256 * s : 256 * (s + 1)], COPY
             )
-        w_bank = [ps.tile([P, PACK, P], F32, name=f"w_bank{h}") for h in range(HALVES)]
+        w_bank = [ps.tile([P, PACK, P], F32, name=f"w_bank{h}", tag=f"w_bank{h}") for h in range(HALVES)]
         for h in range(HALVES):
             turn(w_bank[h], lambda t: score[h][:, t:I:PACK], True, False)
 
         v_bank = [ps.tile([P, PACK, P], F32, name=f"v_bank{j}", tag=f"v_bank{j}") for j in range(PACK)]
-        v_codes = tile([P, E], U32, "v_codes")
         v_scales = tile([P, E], U8, "v_scales")
 
-        diff = []
-
         def gather_values(j):
-            second = tile([P, I], F32, f"second{j}")
-            nc.scalar.activation(second[:], v2_pool[j][:].indirect(by_col[:]), COPY)
-            diff.append(tile([P, I], F32, f"diff{j}", "places0" if j == 0 else None))
-            nc.vector.tensor_tensor(diff[j][:], v1_pool[j][:].indirect(by_tok[:]), second[:], SUBTRACT)
+            neg2 = tile([P, I], F32, f"neg2_{j}")
+            nc.scalar.activation(neg2[:], v2_pool[j][:].indirect(by_col[:]), COPY, scale=-1.0)
+            turn(v_bank[j], lambda t: neg2[:, t:I:PACK], True, False)
+            pos1 = tile([P, PACK, P], F32, f"pos1_{j}", "places0" if j == 0 else None)
+            nc.vector.tensor_copy(pos1[:].rearrange("p t s -> p s t"), v1_pool[j][:].indirect(by_tok[:]))
+            turn(v_bank[j], lambda t: pos1[:, t, :], False, True)
 
-        def turn_values(j0, j1, over):
-            apart = tile([P, j1 - j0, PACK, P], F32, f"apart{j0}", over)
+        def absolute(apart, j0, j1):
             for j in range(j0, j1):
                 nc.scalar.activation(
-                    apart[:, j - j0].rearrange("p t s -> p s t"), diff[j][:].rearrange("p (s t) -> p s t", t=PACK), ABS
+                    apart[:, (j - j0) * P : (j - j0 + 1) * P, :], v_bank[j][:].rearrange("p t m -> p m t"), ABS
                 )
-                turn(v_bank[j], lambda t: apart[:, j - j0, t, :], True, True)
 
-        def quantise_values(j0, j1):
-            v_bf = tile([P, (j1 - j0) * P, PACK], BF16, f"v_bf{j0}", "v1_pool3")
-            for j in range(j0, j1):
-                nc.vector.tensor_tensor(
-                    v_bf[:, (j - j0) * P : (j - j0 + 1) * P, :], v_bank[j][:].rearrange("p t m -> p m t"),
-                    v_fac[:].unsqueeze(1).to_broadcast([P, P, PACK]), MULT,
-                )
+        def scale_values(engine, v_bf, apart):
+            engine.tensor_tensor(v_bf, apart, v_fac[:].unsqueeze(1).to_broadcast(list(apart.shape)), MULT)
+
+        def quantise_values(codes, v_bf, j0, j1):
             nc.vector.quantize_mx(
-                out=v_codes[:, j0 * P : j1 * P].bitcast(FP8X4), scales=v_scales[:, j0 * P : j1 * P],
-                in_=v_bf[:].rearrange("p m t -> p (m t)"),
+                out=codes.bitcast(FP8X4), scales=v_scales[:, j0 * P : j1 * P], in_=v_bf.rearrange("p m t -> p (m t)")
             )
 
         found0 = tile([P, PACK, P], F32, "found0")
@@ -155,23 +150,38 @@ def tile_attend_passedthrough_apartvalues_lean_pl_kernel(
         found1 = tile([P, I], F32, "found1")
         nc.scalar.activation(found1[:], places[1][:].indirect(look_at[:]), COPY)
         turn(w_bank[1], lambda t: found1[:, t:I:PACK], False, True)
-
         gather_values(0)
         gather_values(1)
-
-        w_bf = tile([P, Q, PACK], BF16, "w_bf")
-        w_codes = tile([P, Q], U32, "w_codes")
-        w_scales = tile([P, Q], U8, "w_scales")
+        w_bf = tile([P, Q, PACK], BF16, "w_bf", "v1_pool1")
         for h in range(HALVES):
             nc.vector.tensor_tensor(
                 w_bf[:, h * P : (h + 1) * P, :], w_bank[h][:].rearrange("p t q -> p q t"),
                 w_fac[:].unsqueeze(1).to_broadcast([P, P, PACK]), MULT,
             )
+        gather_values(2)
+        gather_values(3)
+
+        apart_01 = tile([P, 2 * P, PACK], F32, "apart_01", "v2_pool3")
+        apart_23 = tile([P, 2 * P, PACK], F32, "apart_23")
+        absolute(apart_01, 0, 2)
+        absolute(apart_23, 2, 4)
+        v_bf01 = tile([P, 2 * P, PACK], BF16, "v_bf01")
+        v_bf23 = last.tile([P, 2 * P, PACK], BF16, name="v_bf23", offset=0, align_bytes=64)
+        v_codes = last.tile([P, E], U32, name="v_codes", offset=2048, align_bytes=64)
+        w_codes = last.tile([P, Q], U32, name="w_codes", offset=4096, align_bytes=64)
+        w_scales = tile([P, Q], U8, "w_scales")
+        scale_values(nc.gpsimd, v_bf01[:, :P, :], apart_01[:, :P, :])
+        scale_values(nc.gpsimd, v_bf01[:, P:, :], apart_01[:, P:, :])
         nc.vector.quantize_mx(
             out=w_codes[:].bitcast(FP8X4), scales=w_scales[:], in_=w_bf[:].rearrange("p q t -> p (q t)")
         )
+        quantise_values(v_codes[:, : 2 * P], v_bf01[:], 0, 2)
+        scale_values(nc.vector, v_bf23[:, :P, :], apart_23[:, :P, :])
+        quantise_values(v_codes[:, 2 * P : 3 * P], v_bf23[:, :P, :], 2, 3)
+        scale_values(nc.vector, v_bf23[:, P:, :], apart_23[:, P:, :])
+        quantise_values(v_codes[:, 3 * P :], v_bf23[:, P:, :], 3, 4)
 
-        out_bank = [ps.tile([P, PACK, P], F32, name=f"out_bank{h}", tag=f"mx_bank{h}") for h in range(HALVES)]
+        out_bank = [ps.tile([P, PACK, P], F32, name=f"out_bank{h}", tag=f"w_bank{h}") for h in range(HALVES)]
 
         def product(j0, j1, h):
             cols = slice(h * P, (h + 1) * P)
@@ -185,13 +195,6 @@ def tile_attend_passedthrough_apartvalues_lean_pl_kernel(
         out_rows = out_0.rearrange("(m j) q -> m j q", j=PACK)
         early = tile([P, 2, Q], F32, "early")
         late = tile([P, 2, Q], F32, "late")
-        gather_values(2)
-        turn_values(0, 1, "v2_pool2")
-        gather_values(3)
-        turn_values(1, 3, "v2_pool3")
-        turn_values(3, 4, None)
-        quantise_values(0, 2)
-        quantise_values(2, 4)
         for h in range(HALVES):
             product(0, 2, h)
             nc.scalar.copy(early[:, :, h * P : (h + 1) * P], out_bank[h][:, :2, :])

@@ -74,11 +74,10 @@ def tile_attend_passedthrough_apartvalues_lean_pl_kernel(
         nc.sync.dma_start(v1_pool[1][:], vals_rows[1])
         w_fac = tile([P, PACK], F32, "w_fac")
         nc.sync.dma_start(w_fac[:], wfac.rearrange("o (p t) -> (o p) t", t=PACK))
-        for j in (2, 3):
-            nc.sync.dma_start(v2_pool[j][:], vals2_rows[j])
         v_fac = tile([P, PACK], F32, "v_fac")
         nc.sync.dma_start(v_fac[:], vsc.rearrange("o (p t) -> (o p) t", t=PACK))
         for j in (2, 3):
+            nc.sync.dma_start(v2_pool[j][:], vals2_rows[j])
             nc.sync.dma_start(v1_pool[j][:], vals_rows[j])
 
         places = [tile([P, Z], F32, f"places{h}") for h in range(HALVES)]
@@ -126,59 +125,60 @@ def tile_attend_passedthrough_apartvalues_lean_pl_kernel(
             neg2 = tile([P, I], F32, f"neg2_{j}")
             nc.scalar.activation(neg2[:], v2_pool[j][:].indirect(by_col[:]), COPY, scale=-1.0)
             turn(v_bank[j], lambda t: neg2[:, t:I:PACK], True, False)
-            pos1 = tile([P, PACK, P], F32, f"pos1_{j}", "places0" if j == 0 else None)
+            pos1 = tile([P, PACK, P], F32, f"pos1_{j}")
             nc.vector.tensor_copy(pos1[:].rearrange("p t s -> p s t"), v1_pool[j][:].indirect(by_tok[:]))
             turn(v_bank[j], lambda t: pos1[:, t, :], False, True)
 
-        def absolute(apart, j0, j1):
-            for j in range(j0, j1):
-                nc.scalar.activation(
-                    apart[:, (j - j0) * P : (j - j0 + 1) * P, :], v_bank[j][:].rearrange("p t m -> p m t"), ABS
-                )
+        def absolute(apart, j, m0, m1):
+            nc.scalar.activation(apart, v_bank[j][:, :, m0:m1].rearrange("p t m -> p m t"), ABS)
 
-        def scale_values(engine, v_bf, apart):
-            engine.tensor_tensor(v_bf, apart, v_fac[:].unsqueeze(1).to_broadcast(list(apart.shape)), MULT)
+        def scale_slots(engine, out, in_, factor):
+            engine.tensor_tensor(out, in_, factor[:].unsqueeze(1).to_broadcast(list(out.shape)), MULT)
 
         def quantise_values(codes, v_bf, j0, j1):
             nc.vector.quantize_mx(
                 out=codes.bitcast(FP8X4), scales=v_scales[:, j0 * P : j1 * P], in_=v_bf.rearrange("p m t -> p (m t)")
             )
 
-        found0 = tile([P, PACK, P], F32, "found0")
-        nc.vector.tensor_copy(found0[:].rearrange("p t s -> p s t"), places[0][:].indirect(look_at[:]))
-        turn(w_bank[0], lambda t: found0[:, t, :], False, True)
         found1 = tile([P, I], F32, "found1")
         nc.scalar.activation(found1[:], places[1][:].indirect(look_at[:]), COPY)
         turn(w_bank[1], lambda t: found1[:, t:I:PACK], False, True)
         gather_values(0)
         gather_values(1)
-        w_bf = tile([P, Q, PACK], BF16, "w_bf", "v1_pool1")
-        for h in range(HALVES):
-            nc.vector.tensor_tensor(
-                w_bf[:, h * P : (h + 1) * P, :], w_bank[h][:].rearrange("p t q -> p q t"),
-                w_fac[:].unsqueeze(1).to_broadcast([P, P, PACK]), MULT,
-            )
+        found0 = tile([P, PACK, P], F32, "found0", "v1_pool1")
+        nc.vector.tensor_copy(found0[:].rearrange("p t s -> p s t"), places[0][:].indirect(look_at[:]))
+        turn(w_bank[0], lambda t: found0[:, t, :], False, True)
+        w_bf = tile([P, Q, PACK], BF16, "w_bf", "places0")
+        scale_slots(nc.vector, w_bf[:, P:, :], w_bank[1][:].rearrange("p t q -> p q t"), w_fac)
         gather_values(2)
-        gather_values(3)
 
-        apart_01 = tile([P, 2 * P, PACK], F32, "apart_01", "v2_pool3")
-        apart_23 = tile([P, 2 * P, PACK], F32, "apart_23")
-        absolute(apart_01, 0, 2)
-        absolute(apart_23, 2, 4)
+        apart_0 = tile([P, P, PACK], F32, "apart_0", "places1")
+        absolute(apart_0[:], 0, 0, P)
+        staged = tile([P, 2, P, PACK], F32, "staged", "v2_pool2")
+        absolute(staged[:, 0], 1, 0, P)
+        nc.scalar.copy(staged[:, 1], w_bank[0][:].rearrange("p t q -> p q t"))
+        gather_values(3)
         v_bf01 = tile([P, 2 * P, PACK], BF16, "v_bf01")
+        scale_slots(nc.gpsimd, v_bf01[:, :P, :], apart_0[:], v_fac)
+        scale_slots(nc.gpsimd, v_bf01[:, P:, :], staged[:, 0], v_fac)
+        scale_slots(nc.gpsimd, w_bf[:, :P, :], staged[:, 1], w_fac)
+
+        apart_23 = tile([P, 2 * P, PACK], F32, "apart_23", "v2_pool3")
+        absolute(apart_23[:, :P, :], 2, 0, P)
+        for m0 in (0, P // 2):
+            absolute(apart_23[:, P + m0 : P + m0 + P // 2, :], 3, m0, m0 + P // 2)
         v_bf23 = last.tile([P, 2 * P, PACK], BF16, name="v_bf23", offset=0, align_bytes=64)
         v_codes = last.tile([P, E], U32, name="v_codes", offset=2048, align_bytes=64)
         w_codes = last.tile([P, Q], U32, name="w_codes", offset=4096, align_bytes=64)
         w_scales = tile([P, Q], U8, "w_scales")
-        scale_values(nc.gpsimd, v_bf01[:, :P, :], apart_01[:, :P, :])
-        scale_values(nc.gpsimd, v_bf01[:, P:, :], apart_01[:, P:, :])
         nc.vector.quantize_mx(
             out=w_codes[:].bitcast(FP8X4), scales=w_scales[:], in_=w_bf[:].rearrange("p q t -> p (q t)")
         )
         quantise_values(v_codes[:, : 2 * P], v_bf01[:], 0, 2)
-        scale_values(nc.vector, v_bf23[:, :P, :], apart_23[:, :P, :])
+        scale_slots(nc.vector, v_bf23[:, :P, :], apart_23[:, :P, :], v_fac)
         quantise_values(v_codes[:, 2 * P : 3 * P], v_bf23[:, :P, :], 2, 3)
-        scale_values(nc.vector, v_bf23[:, P:, :], apart_23[:, P:, :])
+        for m0 in (P, P + P // 2):
+            scale_slots(nc.vector, v_bf23[:, m0 : m0 + P // 2, :], apart_23[:, m0 : m0 + P // 2, :], v_fac)
         quantise_values(v_codes[:, 3 * P :], v_bf23[:, P:, :], 3, 4)
 
         out_bank = [ps.tile([P, PACK, P], F32, name=f"out_bank{h}", tag=f"w_bank{h}") for h in range(HALVES)]

from contextlib import ExitStack

import concourse.mybir as mybir
from concourse.masks import make_identity

D, T, I, Q, E, Z, X = 512, 2048, 512, 256, 512, 1024, 1024
FLOPS = 2 * D * Q * I + 2 * I * E * Q

F32 = mybir.dt.float32
BF16 = mybir.dt.bfloat16
I32 = mybir.dt.int32
U32 = mybir.dt.uint32
U16 = mybir.dt.uint16
U8 = mybir.dt.uint8
FP8X4 = mybir.dt.float8_e4m3fn_x4
FP4X4 = mybir.dt.float4_e2m1fn_x4
MULT = mybir.AluOpType.mult
COPY = mybir.ActivationFunctionType.Copy
ABS = mybir.ActivationFunctionType.Abs

P = 128
PACK = 4
HALVES = Q // P


def tile_attend_passedthrough_apartvalues_lean_pl_kernel(
    tc, query, keys_words, keys_scales, wfac, vals, vals2, vsc, offs, offs2, offs3, offs4, out_0, out_1, out_2
):
    nc = tc.nc
    with ExitStack() as ctx:
        sb = ctx.enter_context(tc.tile_pool(name="sb", bufs=1))
        last = ctx.enter_context(tc.tile_pool(name="last", bufs=1))
        ps = ctx.enter_context(tc.psum_pool(name="ps", bufs=1))

        def tile(shape, dtype, name, over=None):
            return sb.tile(shape, dtype, name=name, tag=over or name, align_bytes=64)

        def load_list(src, name):
            lst = tile([P, I // 16], U16, name)
            nc.sync.dma_start(lst[:], src)
            return lst

        def turn(bank, src_of, first, last):
            for t in range(PACK):
                nc.tensor.matmul(
                    bank[:, t, :], lhsT=src_of(t), rhs=ident[:], is_transpose=True,
                    start=(first and t == 0), stop=(last and t == PACK - 1),
                )

        ks_pool = tile([P, T], U8, "ks_pool")
        nc.vector.memset(ks_pool[:].bitcast(U32), 0)
        by_tok = load_list(offs, "by_tok")
        kw_pool = tile([P, T], U16, "kw_pool")
        nc.sync.dma_start(kw_pool[:].bitcast(I32), keys_words[0].bitcast(I32))
        for quad in range(4):
            nc.sync.dma_start(
                ks_pool[32 * quad : 32 * quad + 4, :].bitcast(I32),
                keys_scales[0, 4 * quad : 4 * quad + 4, :].bitcast(I32),
            )
        q_raw = tile([P, PACK, Q], F32, "q_raw")
        nc.sync.dma_start(q_raw[:], query.rearrange("(p t) q -> p t q", t=PACK))

        vals_rows = vals.rearrange("(m j) c -> j m c", j=PACK)
        vals2_rows = vals2.rearrange("(m j) c -> j m c", j=PACK)
        v1_pool = [tile([P, T], F32, f"v1_pool{j}") for j in range(PACK - 1)]
        v1_pool.append(last.tile([P, T], F32, name="v1_pool3", offset=0, align_bytes=64))
        v2_pool = [tile([P, X], F32, f"v2_pool{j}") for j in range(PACK)]
        by_col = load_list(offs4, "by_col")
        nc.sync.dma_start(v2_pool[0][:], vals2_rows[0])
        nc.sync.dma_start(v2_pool[1][:], vals2_rows[1])
        put_at = load_list(offs2, "put_at")
        nc.sync.dma_start(v1_pool[0][:], vals_rows[0])
        look_at = load_list(offs3, "look_at")
        nc.sync.dma_start(v1_pool[1][:], vals_rows[1])
        w_fac = tile([P, PACK], F32, "w_fac")
        nc.sync.dma_start(w_fac[:], wfac.rearrange("o (p t) -> (o p) t", t=PACK))
        v_fac = tile([P, PACK], F32, "v_fac")
        nc.sync.dma_start(v_fac[:], vsc.rearrange("o (p t) -> (o p) t", t=PACK))
        for j in (2, 3):
            nc.sync.dma_start(v2_pool[j][:], vals2_rows[j])
            nc.sync.dma_start(v1_pool[j][:], vals_rows[j])

        places = [tile([P, Z], F32, f"places{h}") for h in range(HALVES)]
        nc.vector.memset(places[0][:], 0.0)
        nc.gpsimd.memset(places[1][:], 0.0)
        ident = tile([P, P], F32, "ident")
        make_identity(nc, ident[:])

        kw = tile([P, I], U16, "kw")
        ks = tile([P, I], U8, "ks")
        q_bf = tile([P, Q, PACK], BF16, "q_bf")
        q_codes = tile([P, Q], U32, "q_codes")
        q_scales = tile([P, Q], U8, "q_scales")
        nc.vector.tensor_copy(kw[:], kw_pool[:].indirect(by_tok[:]))
        nc.vector.tensor_copy(ks[:], ks_pool[:].indirect(by_tok[:]))
        score_bank = [ps.tile([P, I], F32, name=f"score_bank{h}", tag=f"v_bank{h}") for h in range(HALVES)]
        score = [tile([P, I], F32, f"score{h}") for h in range(HALVES)]
        for h in range(HALVES):
            cols = slice(h * P, (h + 1) * P)
            nc.scalar.copy(q_bf[:, cols, :], q_raw[:, :, cols].rearrange("p t q -> p q t"))
            nc.vector.quantize_mx(
                out=q_codes[:, cols].bitcast(FP8X4), scales=q_scales[:, cols],
                in_=q_bf[:, cols, :].rearrange("p q t -> p (q t)"),
            )
            nc.tensor.matmul_mx(
                out=score_bank[h][:], lhsT=q_codes[:, cols].bitcast(FP8X4), lhsT_scale=q_scales[:, cols],
                rhs=kw[:].bitcast(FP4X4), rhs_scale=ks[:], start=True, stop=True,
            )
        nc.vector.tensor_copy(score[0][:], score_bank[0][:])
        nc.vector.tensor_copy(score[1][:], score_bank[1][:])

        nc.vector.tensor_copy(places[0][:].indirect(put_at[:]), score[0][:])
        for s in range(2):
            nc.scalar.activation(
                places[1][:].indirect(put_at[:, 16 * s : 16 * (s + 1)]), score[1][:, 256 * s : 256 * (s + 1)], COPY
            )
        w_bank = [ps.tile([P, PACK, P], F32, name=f"w_bank{h}", tag=f"w_bank{h}") for h in range(HALVES)]
        for h in range(HALVES):
            turn(w_bank[h], lambda t: score[h][:, t:I:PACK], True, False)

        v_bank = [ps.tile([P, PACK, P], F32, name=f"v_bank{j}", tag=f"v_bank{j}") for j in range(PACK)]
        v_scales = tile([P, E], U8, "v_scales")

        def gather_values(j):
            neg2 = tile([P, I], F32, f"neg2_{j}")
            nc.scalar.activation(neg2[:], v2_pool[j][:].indirect(by_col[:]), COPY, scale=-1.0)
            turn(v_bank[j], lambda t: neg2[:, t:I:PACK], True, False)
            pos1 = tile([P, PACK, P], F32, f"pos1_{j}")
            nc.vector.tensor_copy(pos1[:].rearrange("p t s -> p s t"), v1_pool[j][:].indirect(by_tok[:]))
            turn(v_bank[j], lambda t: pos1[:, t, :], False, True)

        def absolute(apart, j, m0, m1):
            nc.scalar.activation(apart, v_bank[j][:, :, m0:m1].rearrange("p t m -> p m t"), ABS)

        def scale_slots(engine, out, in_, factor):
            engine.tensor_tensor(out, in_, factor[:].unsqueeze(1).to_broadcast(list(out.shape)), MULT)

        def quantise_values(codes, v_bf, j0, j1):
            nc.vector.quantize_mx(
                out=codes.bitcast(FP8X4), scales=v_scales[:, j0 * P : j1 * P], in_=v_bf.rearrange("p m t -> p (m t)")
            )

        found1 = tile([P, I], F32, "found1")
        nc.scalar.activation(found1[:], places[1][:].indirect(look_at[:]), COPY)
        turn(w_bank[1], lambda t: found1[:, t:I:PACK], False, True)
        gather_values(0)
        gather_values(1)
        found0 = tile([P, PACK, P], F32, "found0", "v1_pool1")
        nc.vector.tensor_copy(found0[:].rearrange("p t s -> p s t"), places[0][:].indirect(look_at[:]))
        turn(w_bank[0], lambda t: found0[:, t, :], False, True)
        w_bf = tile([P, Q, PACK], BF16, "w_bf", "places0")
        scale_slots(nc.vector, w_bf[:, P:, :], w_bank[1][:].rearrange("p t q -> p q t"), w_fac)
        gather_values(2)

        apart_0 = tile([P, P, PACK], F32, "apart_0", "places1")
        absolute(apart_0[:], 0, 0, P)
        staged = tile([P, 2, P, PACK], F32, "staged", "v2_pool2")
        absolute(staged[:, 0], 1, 0, P)
        nc.scalar.copy(staged[:, 1], w_bank[0][:].rearrange("p t q -> p q t"))
        gather_values(3)
        v_bf01 = tile([P, 2 * P, PACK], BF16, "v_bf01")
        scale_slots(nc.gpsimd, v_bf01[:, :P, :], apart_0[:], v_fac)
        scale_slots(nc.gpsimd, v_bf01[:, P:, :], staged[:, 0], v_fac)
        scale_slots(nc.gpsimd, w_bf[:, :P, :], staged[:, 1], w_fac)

        apart_23 = tile([P, 2 * P, PACK], F32, "apart_23", "v2_pool3")
        absolute(apart_23[:, :P, :], 2, 0, P)
        for m0 in (0, P // 2):
            absolute(apart_23[:, P + m0 : P + m0 + P // 2, :], 3, m0, m0 + P // 2)
        v_bf23 = last.tile([P, 2 * P, PACK], BF16, name="v_bf23", offset=0, align_bytes=64)
        v_codes = last.tile([P, E], U32, name="v_codes", offset=2048, align_bytes=64)
        w_codes = last.tile([P, Q], U32, name="w_codes", offset=4096, align_bytes=64)
        w_scales = tile([P, Q], U8, "w_scales")
        nc.vector.quantize_mx(
            out=w_codes[:].bitcast(FP8X4), scales=w_scales[:], in_=w_bf[:].rearrange("p q t -> p (q t)")
        )
        quantise_values(v_codes[:, : 2 * P], v_bf01[:], 0, 2)
        scale_slots(nc.vector, v_bf23[:, :P, :], apart_23[:, :P, :], v_fac)
        quantise_values(v_codes[:, 2 * P : 3 * P], v_bf23[:, :P, :], 2, 3)
        for m0 in (P, P + P // 2):
            scale_slots(nc.vector, v_bf23[:, m0 : m0 + P // 2, :], apart_23[:, m0 : m0 + P // 2, :], v_fac)
        quantise_values(v_codes[:, 3 * P :], v_bf23[:, P:, :], 3, 4)

        out_bank = [ps.tile([P, PACK, P], F32, name=f"out_bank{h}", tag=f"w_bank{h}") for h in range(HALVES)]

        def product(j0, j1, h):
            cols = slice(h * P, (h + 1) * P)
            for j in range(j0, j1):
                nc.tensor.matmul_mx(
                    out=out_bank[h][:, j, :], lhsT=v_codes[:, j * P : (j + 1) * P].bitcast(FP8X4),
                    lhsT_scale=v_scales[:, j * P : (j + 1) * P],
                    rhs=w_codes[:, cols].bitcast(FP8X4), rhs_scale=w_scales[:, cols], start=True, stop=True,
                )

        out_rows = out_0.rearrange("(m j) q -> m j q", j=PACK)
        early = tile([P, 2, Q], F32, "early")
        late = tile([P, 2, Q], F32, "late")
        for h in range(HALVES):
            product(0, 2, h)
            nc.scalar.copy(early[:, :, h * P : (h + 1) * P], out_bank[h][:, :2, :])
        nc.sync.dma_start(out_rows[:, :2, :], early[:])
        for h in range(HALVES):
            product(2, 4, h)

        o_bf = tile([P, Q, PACK], BF16, "o_bf")
        o_codes = tile([P, Q], U32, "o_codes")
        o_scales = tile([P, Q], U8, "o_scales")
        nc.vector.tensor_copy(o_bf[:, :P, :], out_bank[0][:].rearrange("p j q -> p q j"))
        nc.scalar.copy(o_bf[:, P:, :], out_bank[1][:].rearrange("p j q -> p q j"))
        nc.vector.tensor_copy(late[:, :, :P], out_bank[0][:, 2:, :])
        nc.scalar.copy(late[:, :, P:], out_bank[1][:, 2:, :])
        nc.vector.quantize_mx(
            out=o_codes[:].bitcast(FP8X4), scales=o_scales[:], in_=o_bf[:].rearrange("p q j -> p (q j)")
        )
        nc.sync.dma_start(out_rows[:, 2:, :], late[:])
        nc.scalar.dma_start(out_1[0].rearrange("p c r -> p (c r)").bitcast(I32), o_codes[:].bitcast(I32))
        for quad in range(4):
            queue = nc.sync if quad < 3 else nc.scalar
            queue.dma_start(
                out_2[0, 4 * quad : 4 * quad + 4, :].bitcast(I32),
                o_scales[32 * quad : 32 * quad + 4, :].bitcast(I32),
            )
